import numpy as np
import ml_dtypes


def mxq(x, axis, fmt="e4m3"):
    dtype, down = {"e4m3": (ml_dtypes.float8_e4m3fn, 7), "e5m2": (ml_dtypes.float8_e5m2, 14)}[fmt]
    v = np.moveaxis(np.asarray(x, np.float32).astype(ml_dtypes.bfloat16).astype(np.float64), axis, -1)
    blocks = v.reshape(v.shape[:-1] + (-1, 32))
    amax = np.abs(blocks).max(-1, keepdims=True)
    byte = np.maximum(np.where(amax > 0, np.frexp(amax)[1] - 1 + 127, 0) - down, 1)
    scale = np.exp2(byte - 127.0)
    codes = (blocks / scale).astype(np.float32).astype(dtype).astype(np.float64)
    return np.moveaxis((codes * scale).reshape(v.shape), -1, axis)


WIDE = False


def mx_kscale(k):
    if not WIDE:
        return np.ones(k)
    levels = np.array([10, -10, 5, -5, 0])
    if k % 512:
        return np.exp2(np.random.permutation(np.resize(levels, k // 32))).repeat(32)
    a = np.empty((k // 512, 16))
    for p in range(k // 512):
        a[p, :8] = np.random.permutation(np.resize(levels, 8))
        for g in range(8):
            far = levels[np.abs(levels - a[p, g]) >= 10]
            a[p, g + 8] = far[np.random.randint(len(far))]
    return np.exp2(a.ravel()).repeat(32)


def f64(x):
    return np.asarray(x).astype(np.float64)


def striped(idx):
    return np.tile(idx.reshape(-1, 16).T, (8, 1)).astype(np.uint16)


def unstriped(offs):
    return offs[:16].T.reshape(-1).astype(np.int64)


def pack_weight(w):
    k, n = w.shape
    w = f64(np.asarray(w, np.float32).astype(ml_dtypes.bfloat16)).reshape(k // 32, 32, n)
    amax = np.abs(w).max(1)
    byte = np.clip(np.where(amax > 0, np.frexp(amax)[1] - 1 + 127 - 7, 1), 1, 254)
    scaled = (w * np.exp2(127.0 - byte)[:, None, :]).reshape(k, n).astype(np.float32)
    words = np.ascontiguousarray(scaled.reshape(k // 512, 128, 4, n).transpose(0, 1, 3, 2)).astype(ml_dtypes.float8_e4m3fn).view(np.uint8)
    return words, np.ascontiguousarray(byte.astype(np.uint8).reshape(k // 512, 16, n))


def unpack_weight(words, scales):
    g, p, n, _ = words.shape
    vals = np.ascontiguousarray(words).view(ml_dtypes.float8_e4m3fn).astype(np.float64) * np.repeat(np.exp2(scales.astype(np.float64) - 127.0), 8, axis=1)[..., None]
    return vals.transpose(0, 1, 3, 2).reshape(g * 512, n)


E2M1 = np.array([0.0, 0.5, 1.0, 1.5, 2.0, 3.0, 4.0, 6.0, -0.0, -0.5, -1.0, -1.5, -2.0, -3.0, -4.0, -6.0])


def pack_fp4(w):
    k, n = w.shape
    w = f64(np.asarray(w, np.float32).astype(ml_dtypes.bfloat16)).reshape(k // 32, 32, n)
    amax = np.abs(w).max(1)
    mant, ex = np.frexp(amax / 6.0)
    byte = np.clip(np.where(amax > 0, np.where(mant > 0.5, ex, ex - 1) + 127, 1), 1, 254)
    scaled = (w * np.exp2(127.0 - byte)[:, None, :]).reshape(k, n).astype(np.float32)
    c = np.ascontiguousarray(scaled.reshape(k // 512, 128, 4, n).transpose(0, 1, 3, 2)).astype(ml_dtypes.float4_e2m1fn).view(np.uint8) & 0xF
    words = (c[..., 0::2] | (c[..., 1::2] << 4)).reshape(k // 512, 128, 2 * n)
    return np.ascontiguousarray(words), np.ascontiguousarray(byte.astype(np.uint8).reshape(k // 512, 16, n))


def unpack_fp4(words, scales):
    g, _, n = scales.shape
    words = np.ascontiguousarray(words).reshape(g, 128, n, 2)
    nib = np.empty((g, 128, n, 4), np.uint8)
    nib[..., 0::2] = words & 0xF
    nib[..., 1::2] = words >> 4
    vals = E2M1[nib] * np.repeat(np.exp2(scales.astype(np.float64) - 127.0), 8, axis=1)[..., None]
    return vals.transpose(0, 1, 3, 2).reshape(g * 512, n)


K, T, S, D, N, H = 1024, 2048, 512, 4, 256, 512


def setup_inputs():
    n = np.random.standard_normal
    s = mx_kscale(K)[:, None]
    u = mx_kscale(H)
    packed_xT = pack_weight(n((K, T)) * s)
    packed_w1 = pack_fp4(n((K, H)) / np.sqrt(K) / s)
    packed_w2 = pack_fp4(n((K, H)) / np.sqrt(K) / s)
    packed_w3 = pack_fp4(n((H, N)) / np.sqrt(H) / u[:, None])
    return {
        "x_words": packed_xT[0],
        "x_scales": packed_xT[1],
        "w1_words": packed_w1[0],
        "w1_scales": packed_w1[1],
        "w2_words": packed_w2[0],
        "w2_scales": packed_w2[1],
        "unit": (np.random.uniform(0.6, 1.4, (H, 1)) * u[:, None]).astype(np.float32),
        "w3_words": packed_w3[0],
        "w3_scales": packed_w3[1],
        "offs": striped(np.random.permutation(T)[:S]),
        "mom": striped(np.random.permutation(S)),
    }


def reference(x_words, x_scales, w1_words, w1_scales, w2_words, w2_scales, unit, w3_words, w3_scales, offs, mom):
    xq = unpack_weight(x_words, x_scales)[:, unstriped(offs)]
    ec = unpack_fp4(w1_words, w1_scales).T @ xq
    eu = unpack_fp4(w2_words, w2_scales).T @ xq
    dlt = ec - eu
    d2 = (dlt) ** 2
    nrm = np.sqrt(d2.reshape(len(d2), -1, D).mean(axis=2) + 0.1)
    dn = dlt / np.repeat(nrm, D, axis=1)
    dc = dn * ec
    cc2 = (ec) ** 2
    proj = (dc.reshape(len(dc), -1, D).sum(axis=2)) / (cc2.reshape(len(cc2), -1, D).sum(axis=2) + 0.3)
    par = np.repeat(proj, D, axis=1) * ec
    gui = ec + 1.5 * (dn - par) + 0.4 * par
    hid = f64(unit) * (gui - (0.7 * dn[:, unstriped(mom)]))
    return unpack_fp4(w3_words, w3_scales).T @ mxq(hid, 0, "e4m3")

@@ -1,0 +1,229 @@
+import math
+from contextlib import ExitStack
+
+import concourse.mybir as mybir
+from concourse.masks import make_identity
+
+K, T, S, D, N, H = 1024, 2048, 512, 4, 256, 512
+FLOPS = 2 * (2 * K * H * S + H * N * S)
+
+F32 = mybir.dt.float32
+BF16 = mybir.dt.bfloat16
+I32 = mybir.dt.int32
+U32 = mybir.dt.uint32
+U16 = mybir.dt.uint16
+U8 = mybir.dt.uint8
+FP8X4 = mybir.dt.float8_e4m3fn_x4
+FP4X4 = mybir.dt.float4_e2m1fn_x4
+ACT = mybir.ActivationFunctionType
+MULT = mybir.AluOpType.mult
+ADD = mybir.AluOpType.add
+
+P = 128
+PACK = 4
+PASSES = K // (P * PACK)
+V = S // D
+HALVES = 2
+SH = S // HALVES
+LIST_COLS = SH // 16
+CHUNKS = 4
+SC = S // CHUNKS
+
+
+def load_scale_rows(queue, tile, scales):
+    for q in range(4):
+        queue.dma_start(
+            out=tile[32 * q : 32 * q + 4, :, :].bitcast(I32),
+            in_=scales[:, 4 * q : 4 * q + 4, :].rearrange("o r c -> r o c").bitcast(I32),
+        )
+
+
+def tile_picked_yapgui_mom_p_kernel(
+    tc, x_words, x_scales, w1_words, w1_scales, w2_words, w2_scales, unit, w3_words, w3_scales, offs, mom, out
+):
+    nc = tc.nc
+    with ExitStack() as ctx:
+        keep = ctx.enter_context(tc.tile_pool(name="keep", bufs=1))
+        psum = ctx.enter_context(tc.psum_pool(name="psum", bufs=1))
+
+        def sb(shape, dtype, name, tag=None):
+            return keep.tile(shape, dtype, name=name, tag=tag or name, align_bytes=64)
+
+        offs_sb = keep.tile([P, S // 16], U16, name="offs_sb")
+        mom_sb = keep.tile([P, S // 16], U16, name="mom_sb")
+        xs_raw = sb([P, PASSES, T], U8, "xs_raw")
+        ws_raw = sb([P, 2, PASSES, H], U8, "ws_raw")
+        ww_raw = sb([P, 2, PASSES, 2 * H], U8, "ww_raw")
+        xw_raw = [sb([P, T], I32, f"xw_raw{o}") for o in range(PASSES)]
+        w3_sb = sb([P, 2 * N], U8, "w3_sb")
+        w3s_sb = sb([P, 1, N], U8, "w3s_sb")
+        unit_sb = sb([P, PACK], F32, "unit_sb")
+        unit15 = sb([P, PACK], F32, "unit15")
+        ident = sb([P, P], F32, "ident")
+
+        def load_words(o):
+            nc.gpsimd.dma_start(out=xw_raw[o][:], in_=x_words[o].rearrange("p c r -> p (c r)").bitcast(I32))
+
+        load_words(0)
+        make_identity(nc, ident[:])
+        nc.gpsimd.memset(w3s_sb[:].rearrange("p o c -> p (o c)").bitcast(I32), 0)
+        nc.gpsimd.dma_start(out=unit_sb[:], in_=unit.rearrange("(p t) o -> p (t o)", t=PACK))
+        load_words(1)
+        nc.vector.memset(xs_raw[:].rearrange("p o c -> p (o c)").bitcast(I32), 0)
+        nc.vector.memset(ws_raw[:].rearrange("p w o c -> p (w o c)").bitcast(I32), 0)
+        nc.sync.dma_start(offs_sb[:], offs)
+        for w, words in enumerate((w1_words, w2_words)):
+            nc.sync.dma_start(out=ww_raw[:, w].bitcast(I32), in_=words.rearrange("o p c -> p o c").bitcast(I32))
+        load_scale_rows(nc.sync, xs_raw, x_scales)
+        load_scale_rows(nc.sync, ws_raw[:, 0], w1_scales)
+        load_scale_rows(nc.sync, ws_raw[:, 1], w2_scales)
+        nc.sync.dma_start(mom_sb[:], mom)
+        nc.gpsimd.dma_start(out=w3_sb[:].bitcast(I32), in_=w3_words[0].bitcast(I32))
+        load_scale_rows(nc.sync, w3s_sb, w3_scales)
+        nc.gpsimd.tensor_scalar(out=unit15[:], in0=unit_sb[:], scalar1=1.5, scalar2=0.0, op0=MULT, op1=ADD)
+
+        xs = [sb([P, S], U8, f"xs{o}") for o in range(PASSES)]
+        xw = {}
+        ww, ws = {}, {}
+        prod = [[psum.tile([P, S], F32, name=f"prod{t}_{w}", tag=f"bank{t}_{w}") for w in range(2)] for t in range(PACK)]
+
+        def deal_words(t):
+            ww[t] = sb([P, 2 * PASSES, 2 * P], U8, f"ww{t}", tag="xw_raw1" if t % 2 else "ww")
+            nc.vector.tensor_copy(
+                out=ww[t][:].rearrange("p g (m b) -> p g m b", b=2),
+                in_=ww_raw[:].rearrange("p w o (m t b) -> p t (w o) m b", t=PACK, b=2)[:, t],
+            )
+
+        def deal_scales(t):
+            ws[t] = sb([P, 2 * PASSES, P], U8, f"ws{t}", tag="xw_raw0" if t % 2 else "ws")
+            nc.vector.tensor_copy(out=ws[t][:], in_=ws_raw[:].rearrange("p w o (m t) -> p t (w o) m", t=PACK)[:, t])
+
+        def multiply(t, w, o):
+            nc.tensor.matmul_mx(
+                out=prod[t][w][:],
+                lhsT=ww[t][:, PASSES * w + o, :].bitcast(FP4X4),
+                lhsT_scale=ws[t][:, PASSES * w + o, :],
+                rhs=xw[o][:].bitcast(FP8X4),
+                rhs_scale=xs[o][:],
+                start=(o == 0),
+                stop=(o == PASSES - 1),
+            )
+
+        def products(t):
+            deal_words(t)
+            deal_scales(t)
+            for w in range(2):
+                for o in range(PASSES):
+                    multiply(t, w, o)
+
+        deal_words(0)
+        for o in range(PASSES):
+            nc.vector.tensor_copy(out=xs[o][:], in_=xs_raw[:, o, :].indirect(offs_sb[:]))
+        for o in range(PASSES):
+            xw[o] = sb([P, S], I32, f"xw{o}", tag="xw1" if o else "xs_raw")
+            nc.vector.tensor_copy(out=xw[o][:].bitcast(U32), in_=xw_raw[o][:].bitcast(U32).indirect(offs_sb[:]))
+            if o == 0:
+                deal_scales(0)
+            for w in range(2):
+                multiply(0, w, o)
+        products(1)
+
+        ec = [sb([P, S], F32, f"ec{t}") for t in range(PACK)]
+        dlt = [sb([P, S], F32, f"dlt{t}") for t in range(PACK)]
+        own = sb([P, PACK, S], F32, "own")
+        fetched = sb([P, PACK, S], F32, "fetched")
+        sums = {}
+
+        def patch(ap):
+            return ap.rearrange("p (v d) -> p v d", d=D)
+
+        def patch_sums(t):
+            terms = [sb([P, D, V], F32, f"terms{t}_{j}") for j in range(3)]
+            nc.scalar.copy(out=ec[t][:], in_=prod[t][0][:])
+            nc.vector.tensor_sub(out=dlt[t][:], in0=ec[t][:], in1=prod[t][1][:])
+            nc.scalar.activation(
+                out=terms[1][:], in_=prod[t][0][:].rearrange("p (v d) -> p d v", d=D), func=ACT.Square, scale=math.sqrt(1 / 3)
+            )
+            nc.scalar.activation(out=terms[0][:].rearrange("p d v -> p v d"), in_=patch(dlt[t][:]), func=ACT.Square, scale=0.5)
+            nc.vector.tensor_mul(out=terms[2][:].rearrange("p d v -> p v d"), in0=patch(dlt[t][:]), in1=patch(ec[t][:]))
+            sums[t] = psum.tile([P, 4, P], F32, name=f"sums{t}", tag=f"bank{t}_1")
+            for j in (1, 2, 0):
+                for d in range(D):
+                    nc.tensor.matmul(
+                        out=sums[t][:, j, :], lhsT=terms[j][:, d, :], rhs=ident[:], is_transpose=True, start=(d == 0), stop=(d == D - 1)
+                    )
+
+        def guide(t):
+            roots = sb([P, 2, P], F32, f"roots{t}")
+            inv = sb([P, P], F32, f"inv{t}")
+            part = sb([P, P], F32, f"part{t}")
+            coef = sb([P, P], F32, f"coef{t}")
+            dn = sb([P, S], F32, f"dn{t}")
+            kept = sb([P, S], F32, f"kept{t}")
+            nc.scalar.activation(out=roots[:], in_=sums[t][:, 0:2, :], func=ACT.Abs_reciprocal_sqrt, bias=0.1)
+            nc.scalar.activation(out=inv[:], in_=roots[:, 1, :], func=ACT.Square, scale=math.sqrt(1.1 / 3))
+            back = psum.tile([P, P], F32, name=f"back{t}", tag=f"bank{t}_0")
+            nc.tensor.transpose(back[:], roots[:, 0, :], ident[:])
+            nc.vector.scalar_tensor_tensor(out=part[:], in0=sums[t][:, 2, :], scalar=-1.0, in1=roots[:, 0, :], op0=MULT, op1=MULT)
+            nc.vector.tensor_mul(out=coef[:], in0=part[:], in1=inv[:])
+            nc.tensor.transpose(sums[t][:, 3, :], coef[:], ident[:])
+            nc.vector.scalar_tensor_tensor(
+                out=patch(dn[:]),
+                in0=back[:].unsqueeze(2).to_broadcast([P, V, D]),
+                scalar=unit15[:, t : t + 1],
+                in1=patch(dlt[t][:]),
+                op0=MULT,
+                op1=MULT,
+            )
+            for h in range(HALVES):
+                nc.scalar.activation(
+                    out=fetched[:, t, h * SH : (h + 1) * SH],
+                    in_=dn[:].indirect(mom_sb[:, h * LIST_COLS : (h + 1) * LIST_COLS]),
+                    func=ACT.Copy,
+                    scale=-0.7 / 1.5,
+                )
+            nc.vector.scalar_tensor_tensor(
+                out=patch(kept[:]),
+                in0=sums[t][:, 3, :].unsqueeze(2).to_broadcast([P, V, D]),
+                scalar=1.0,
+                in1=patch(ec[t][:]),
+                op0=ADD,
+                op1=MULT,
+            )
+            nc.vector.scalar_tensor_tensor(
+                out=own[:, t, :], in0=kept[:], scalar=unit_sb[:, t : t + 1], in1=dn[:], op0=MULT, op1=ADD
+            )
+
+        patch_sums(0)
+        for t in range(PACK):
+            if t + 2 < PACK:
+                products(t + 2)
+            if t + 1 < PACK:
+                patch_sums(t + 1)
+            guide(t)
+
+        for h in range(CHUNKS):
+            cols = slice(h * SC, (h + 1) * SC)
+            hid = sb([P, SC, PACK], BF16, f"hid{h}")
+            codes = sb([P, SC], U32, f"codes{h}")
+            scales = sb([P, SC], U8, f"scales{h}")
+            res = sb([P, N // P, SC], F32, f"res{h}")
+            nc.vector.tensor_add(
+                out=hid[:].rearrange("p (c i) t -> p c t i", i=4),
+                in0=own[:, :, cols].rearrange("p t (c i) -> p c t i", i=4),
+                in1=fetched[:, :, cols].rearrange("p t (c i) -> p c t i", i=4),
+            )
+            nc.vector.quantize_mx(out=codes[:].bitcast(FP8X4), scales=scales[:], in_=hid[:].rearrange("p c t -> p (c t)"))
+            acc = psum.tile([P, N // P, SC], F32, name=f"acc{h}", tag=f"bank{h}_0")
+            for m in range(N // P):
+                nc.tensor.matmul_mx(
+                    out=acc[:, m, :],
+                    lhsT=w3_sb[:, 2 * P * m : 2 * P * (m + 1)].bitcast(FP4X4),
+                    lhsT_scale=w3s_sb[:, 0, P * m : P * (m + 1)],
+                    rhs=codes[:].bitcast(FP8X4),
+                    rhs_scale=scales[:],
+                    start=True,
+                    stop=True,
+                )
+            nc.scalar.copy(out=res[:], in_=acc[:])
+            nc.sync.dma_start(out=out.rearrange("(m p) j -> p m j", p=P)[:, :, cols], in_=res[:])

@@ -44,6 +44,7 @@ def tile_picked_yapgui_mom_p_kernel(
     nc = tc.nc
     with ExitStack() as ctx:
         keep = ctx.enter_context(tc.tile_pool(name="keep", bufs=1))
+        reused = ctx.enter_context(tc.tile_pool(name="reused", bufs=1))
         psum = ctx.enter_context(tc.psum_pool(name="psum", bufs=1))
 
         def sb(shape, dtype, name, tag=None):
@@ -51,30 +52,35 @@ def tile_picked_yapgui_mom_p_kernel(
 
         offs_sb = keep.tile([P, S // 16], U16, name="offs_sb")
         mom_sb = keep.tile([P, S // 16], U16, name="mom_sb")
-        xs_raw = sb([P, PASSES, T], U8, "xs_raw")
+        xs_raw = sb([P, T], U8, "xs_raw")
         ws_raw = sb([P, 2, PASSES, H], U8, "ws_raw")
         ww_raw = sb([P, 2, PASSES, 2 * H], U8, "ww_raw")
-        xw_raw = [sb([P, T], I32, f"xw_raw{o}") for o in range(PASSES)]
+        xw_raw = [sb([P, T], I32, "xw_raw0"), reused.tile([P, T], I32, name="xw_raw1", align_bytes=64, offset=0)]
+        xs = [sb([P, S], U8, f"xs{o}") for o in range(PASSES)]
         w3_sb = sb([P, 2 * N], U8, "w3_sb")
         w3s_sb = sb([P, 1, N], U8, "w3s_sb")
         unit_sb = sb([P, PACK], F32, "unit_sb")
         unit15 = sb([P, PACK], F32, "unit15")
         ident = sb([P, P], F32, "ident")
+        warm = sb([P, 1], F32, "warm")
 
         def load_words(o):
             nc.gpsimd.dma_start(out=xw_raw[o][:], in_=x_words[o].rearrange("p c r -> p (c r)").bitcast(I32))
 
         load_words(0)
         make_identity(nc, ident[:])
+        nc.scalar.activation(out=warm[:], in_=ident[:, 0:1], func=ACT.Abs_reciprocal_sqrt, bias=0.1)
         nc.gpsimd.memset(w3s_sb[:].rearrange("p o c -> p (o c)").bitcast(I32), 0)
-        nc.gpsimd.dma_start(out=unit_sb[:], in_=unit.rearrange("(p t) o -> p (t o)", t=PACK))
+        nc.gpsimd.memset(xs[1][:].bitcast(I32), 0)
         load_words(1)
-        nc.vector.memset(xs_raw[:].rearrange("p o c -> p (o c)").bitcast(I32), 0)
+        nc.gpsimd.dma_start(out=unit_sb[:], in_=unit.rearrange("(p t) o -> p (t o)", t=PACK))
+        nc.vector.memset(xs_raw[:].bitcast(I32), 0)
         nc.vector.memset(ws_raw[:].rearrange("p w o c -> p (w o c)").bitcast(I32), 0)
         nc.sync.dma_start(offs_sb[:], offs)
         for w, words in enumerate((w1_words, w2_words)):
             nc.sync.dma_start(out=ww_raw[:, w].bitcast(I32), in_=words.rearrange("o p c -> p o c").bitcast(I32))
-        load_scale_rows(nc.sync, xs_raw, x_scales)
+        for q in range(4):
+            nc.sync.dma_start(out=xs_raw[32 * q : 32 * q + 8, :].bitcast(I32), in_=x_scales[:, 4 * q : 4 * q + 4, :].bitcast(I32))
         load_scale_rows(nc.sync, ws_raw[:, 0], w1_scales)
         load_scale_rows(nc.sync, ws_raw[:, 1], w2_scales)
         nc.sync.dma_start(mom_sb[:], mom)
@@ -82,27 +88,27 @@ def tile_picked_yapgui_mom_p_kernel(
         load_scale_rows(nc.sync, w3s_sb, w3_scales)
         nc.gpsimd.tensor_scalar(out=unit15[:], in0=unit_sb[:], scalar1=1.5, scalar2=0.0, op0=MULT, op1=ADD)
 
-        xs = [sb([P, S], U8, f"xs{o}") for o in range(PASSES)]
         xw = {}
-        ww, ws = {}, {}
+        ww = {}
+        ws = sb([P, PACK, 2 * PASSES, P], U8, "ws")
         prod = [[psum.tile([P, S], F32, name=f"prod{t}_{w}", tag=f"bank{t}_{w}") for w in range(2)] for t in range(PACK)]
 
         def deal_words(t):
-            ww[t] = sb([P, 2 * PASSES, 2 * P], U8, f"ww{t}", tag="xw_raw1" if t % 2 else "ww")
+            shape = [P, 2 * PASSES, 2 * P]
+            if t == 0:
+                ww[t] = sb(shape, U8, f"ww{t}")
+            else:
+                ww[t] = reused.tile(shape, U8, name=f"ww{t}", align_bytes=64, offset=t * 2 * PASSES * 2 * P)
             nc.vector.tensor_copy(
                 out=ww[t][:].rearrange("p g (m b) -> p g m b", b=2),
                 in_=ww_raw[:].rearrange("p w o (m t b) -> p t (w o) m b", t=PACK, b=2)[:, t],
             )
 
-        def deal_scales(t):
-            ws[t] = sb([P, 2 * PASSES, P], U8, f"ws{t}", tag="xw_raw0" if t % 2 else "ws")
-            nc.vector.tensor_copy(out=ws[t][:], in_=ws_raw[:].rearrange("p w o (m t) -> p t (w o) m", t=PACK)[:, t])
-
         def multiply(t, w, o):
             nc.tensor.matmul_mx(
                 out=prod[t][w][:],
                 lhsT=ww[t][:, PASSES * w + o, :].bitcast(FP4X4),
-                lhsT_scale=ws[t][:, PASSES * w + o, :],
+                lhsT_scale=ws[:, t, PASSES * w + o, :],
                 rhs=xw[o][:].bitcast(FP8X4),
                 rhs_scale=xs[o][:],
                 start=(o == 0),
@@ -110,29 +116,33 @@ def tile_picked_yapgui_mom_p_kernel(
             )
 
         def products(t):
-            deal_words(t)
-            deal_scales(t)
             for w in range(2):
                 for o in range(PASSES):
                     multiply(t, w, o)
 
-        deal_words(0)
-        for o in range(PASSES):
-            nc.vector.tensor_copy(out=xs[o][:], in_=xs_raw[:, o, :].indirect(offs_sb[:]))
-        for o in range(PASSES):
-            xw[o] = sb([P, S], I32, f"xw{o}", tag="xw1" if o else "xs_raw")
+        def gather_words(o, tag):
+            xw[o] = sb([P, S], I32, f"xw{o}", tag=tag)
             nc.vector.tensor_copy(out=xw[o][:].bitcast(U32), in_=xw_raw[o][:].bitcast(U32).indirect(offs_sb[:]))
-            if o == 0:
-                deal_scales(0)
+
+        deal_words(0)
+        nc.vector.tensor_copy(out=xs[0][:], in_=xs_raw[:].indirect(offs_sb[:]))
+        for q in range(4):
+            nc.scalar.dma_start(out=xs[1][32 * q : 32 * q + 4, :].bitcast(I32), in_=xs[0][32 * q + 4 : 32 * q + 8, :].bitcast(I32))
+        gather_words(0, "xs_raw")
+        nc.vector.tensor_copy(out=ws[:], in_=ws_raw[:].rearrange("p w o (m t) -> p t (w o) m", t=PACK))
+        gather_words(1, "ws_raw")
+        for o in range(PASSES):
             for w in range(2):
                 multiply(0, w, o)
-        products(1)
+        for t in range(1, PACK):
+            deal_words(t)
+            products(t)
 
         ec = [sb([P, S], F32, f"ec{t}") for t in range(PACK)]
         dlt = [sb([P, S], F32, f"dlt{t}") for t in range(PACK)]
         own = sb([P, PACK, S], F32, "own")
         fetched = sb([P, PACK, S], F32, "fetched")
-        sums = {}
+        sums, back = {}, {}
 
         def patch(ap):
             return ap.rearrange("p (v d) -> p v d", d=D)
@@ -153,23 +163,25 @@ def tile_picked_yapgui_mom_p_kernel(
                         out=sums[t][:, j, :], lhsT=terms[j][:, d, :], rhs=ident[:], is_transpose=True, start=(d == 0), stop=(d == D - 1)
                     )
 
-        def guide(t):
+        def factors(t):
             roots = sb([P, 2, P], F32, f"roots{t}")
             inv = sb([P, P], F32, f"inv{t}")
             part = sb([P, P], F32, f"part{t}")
             coef = sb([P, P], F32, f"coef{t}")
-            dn = sb([P, S], F32, f"dn{t}")
-            kept = sb([P, S], F32, f"kept{t}")
             nc.scalar.activation(out=roots[:], in_=sums[t][:, 0:2, :], func=ACT.Abs_reciprocal_sqrt, bias=0.1)
             nc.scalar.activation(out=inv[:], in_=roots[:, 1, :], func=ACT.Square, scale=math.sqrt(1.1 / 3))
-            back = psum.tile([P, P], F32, name=f"back{t}", tag=f"bank{t}_0")
-            nc.tensor.transpose(back[:], roots[:, 0, :], ident[:])
+            back[t] = psum.tile([P, P], F32, name=f"back{t}", tag=f"bank{t}_0")
+            nc.tensor.transpose(back[t][:], roots[:, 0, :], ident[:])
             nc.vector.scalar_tensor_tensor(out=part[:], in0=sums[t][:, 2, :], scalar=-1.0, in1=roots[:, 0, :], op0=MULT, op1=MULT)
             nc.vector.tensor_mul(out=coef[:], in0=part[:], in1=inv[:])
             nc.tensor.transpose(sums[t][:, 3, :], coef[:], ident[:])
+
+        def guide(t):
+            dn = sb([P, S], F32, f"dn{t}")
+            kept = sb([P, S], F32, f"kept{t}")
             nc.vector.scalar_tensor_tensor(
                 out=patch(dn[:]),
-                in0=back[:].unsqueeze(2).to_broadcast([P, V, D]),
+                in0=back[t][:].unsqueeze(2).to_broadcast([P, V, D]),
                 scalar=unit15[:, t : t + 1],
                 in1=patch(dlt[t][:]),
                 op0=MULT,
@@ -194,12 +206,14 @@ def tile_picked_yapgui_mom_p_kernel(
                 out=own[:, t, :], in0=kept[:], scalar=unit_sb[:, t : t + 1], in1=dn[:], op0=MULT, op1=ADD
             )
 
-        patch_sums(0)
-        for t in range(PACK):
-            if t + 2 < PACK:
-                products(t + 2)
-            if t + 1 < PACK:
-                patch_sums(t + 1)
+        for t in range(PACK + 1):
+            if t < PACK:
+                patch_sums(t)
+            if t == PACK:
+                guide(0)
+            if t > 0:
+                factors(t - 1)
+        for t in range(1, PACK):
             guide(t)
 
         for h in range(CHUNKS):

@@ -55,13 +55,11 @@ def tile_picked_yapgui_mom_p_kernel(
         xs_raw = sb([P, T], U8, "xs_raw")
         ws_raw = sb([P, 2, PASSES, H], U8, "ws_raw")
         ww_raw = sb([P, 2, PASSES, 2 * H], U8, "ww_raw")
-        xw_raw = [sb([P, T], I32, "xw_raw0"), reused.tile([P, T], I32, name="xw_raw1", align_bytes=64, offset=0)]
+        xw_raw = [reused.tile([P, T], I32, name=f"xw_raw{o}", align_bytes=64, offset=4 * T * o) for o in range(PASSES)]
         xs = [sb([P, S], U8, f"xs{o}") for o in range(PASSES)]
-        w3_sb = sb([P, 2 * N], U8, "w3_sb")
-        w3s_sb = sb([P, 1, N], U8, "w3s_sb")
-        unit_sb = sb([P, PACK], F32, "unit_sb")
         unit15 = sb([P, PACK], F32, "unit15")
         ident = sb([P, P], F32, "ident")
+        ones = sb([P, P], F32, "ones")
         warm = sb([P, 1], F32, "warm")
 
         def load_words(o):
@@ -70,10 +68,9 @@ def tile_picked_yapgui_mom_p_kernel(
         load_words(0)
         make_identity(nc, ident[:])
         nc.scalar.activation(out=warm[:], in_=ident[:, 0:1], func=ACT.Abs_reciprocal_sqrt, bias=0.1)
-        nc.gpsimd.memset(w3s_sb[:].rearrange("p o c -> p (o c)").bitcast(I32), 0)
+        nc.gpsimd.memset(ones[:], 1.0)
         nc.gpsimd.memset(xs[1][:].bitcast(I32), 0)
         load_words(1)
-        nc.gpsimd.dma_start(out=unit_sb[:], in_=unit.rearrange("(p t) o -> p (t o)", t=PACK))
         nc.vector.memset(xs_raw[:].bitcast(I32), 0)
         nc.vector.memset(ws_raw[:].rearrange("p w o c -> p (w o c)").bitcast(I32), 0)
         nc.sync.dma_start(offs_sb[:], offs)
@@ -84,9 +81,6 @@ def tile_picked_yapgui_mom_p_kernel(
         load_scale_rows(nc.sync, ws_raw[:, 0], w1_scales)
         load_scale_rows(nc.sync, ws_raw[:, 1], w2_scales)
         nc.sync.dma_start(mom_sb[:], mom)
-        nc.gpsimd.dma_start(out=w3_sb[:].bitcast(I32), in_=w3_words[0].bitcast(I32))
-        load_scale_rows(nc.sync, w3s_sb, w3_scales)
-        nc.gpsimd.tensor_scalar(out=unit15[:], in0=unit_sb[:], scalar1=1.5, scalar2=0.0, op0=MULT, op1=ADD)
 
         xw = {}
         ww = {}
@@ -98,7 +92,7 @@ def tile_picked_yapgui_mom_p_kernel(
             if t == 0:
                 ww[t] = sb(shape, U8, f"ww{t}")
             else:
-                ww[t] = reused.tile(shape, U8, name=f"ww{t}", align_bytes=64, offset=t * 2 * PASSES * 2 * P)
+                ww[t] = reused.tile(shape, U8, name=f"ww{t}", align_bytes=64, offset=4 * T + t * 2 * PASSES * 2 * P)
             nc.vector.tensor_copy(
                 out=ww[t][:].rearrange("p g (m b) -> p g m b", b=2),
                 in_=ww_raw[:].rearrange("p w o (m t b) -> p t (w o) m b", t=PACK, b=2)[:, t],
@@ -116,6 +110,7 @@ def tile_picked_yapgui_mom_p_kernel(
             )
 
         def products(t):
+            deal_words(t)
             for w in range(2):
                 for o in range(PASSES):
                     multiply(t, w, o)
@@ -129,14 +124,19 @@ def tile_picked_yapgui_mom_p_kernel(
         for q in range(4):
             nc.scalar.dma_start(out=xs[1][32 * q : 32 * q + 4, :].bitcast(I32), in_=xs[0][32 * q + 4 : 32 * q + 8, :].bitcast(I32))
         gather_words(0, "xs_raw")
+        unit_sb = reused.tile([P, PACK], F32, name="unit_sb", align_bytes=64, offset=0)
+        w3_sb = reused.tile([P, 2 * N], U8, name="w3_sb", align_bytes=64, offset=64)
+        w3s_sb = reused.tile([P, 1, N], U8, name="w3s_sb", align_bytes=64, offset=64 + 2 * N)
+        nc.sync.dma_start(out=unit_sb[:], in_=unit.rearrange("(p t) o -> p (t o)", t=PACK))
+        nc.sync.dma_start(out=w3_sb[:].bitcast(I32), in_=w3_words[0].bitcast(I32))
+        nc.gpsimd.memset(w3s_sb[:].rearrange("p o c -> p (o c)").bitcast(I32), 0)
+        load_scale_rows(nc.sync, w3s_sb, w3_scales)
+        nc.gpsimd.tensor_scalar(out=unit15[:], in0=unit_sb[:], scalar1=1.5, scalar2=0.0, op0=MULT, op1=ADD)
         nc.vector.tensor_copy(out=ws[:], in_=ws_raw[:].rearrange("p w o (m t) -> p t (w o) m", t=PACK))
         gather_words(1, "ws_raw")
         for o in range(PASSES):
             for w in range(2):
                 multiply(0, w, o)
-        for t in range(1, PACK):
-            deal_words(t)
-            products(t)
 
         ec = [sb([P, S], F32, f"ec{t}") for t in range(PACK)]
         dlt = [sb([P, S], F32, f"dlt{t}") for t in range(PACK)]
@@ -147,10 +147,12 @@ def tile_picked_yapgui_mom_p_kernel(
         def patch(ap):
             return ap.rearrange("p (v d) -> p v d", d=D)
 
-        def patch_sums(t):
-            terms = [sb([P, D, V], F32, f"terms{t}_{j}") for j in range(3)]
+        def difference(t):
             nc.scalar.copy(out=ec[t][:], in_=prod[t][0][:])
             nc.vector.tensor_sub(out=dlt[t][:], in0=ec[t][:], in1=prod[t][1][:])
+
+        def patch_sums(t):
+            terms = [sb([P, D, V], F32, f"terms{t}_{j}") for j in range(3)]
             nc.scalar.activation(
                 out=terms[1][:], in_=prod[t][0][:].rearrange("p (v d) -> p d v", d=D), func=ACT.Square, scale=math.sqrt(1 / 3)
             )
@@ -174,7 +176,8 @@ def tile_picked_yapgui_mom_p_kernel(
             nc.tensor.transpose(back[t][:], roots[:, 0, :], ident[:])
             nc.vector.scalar_tensor_tensor(out=part[:], in0=sums[t][:, 2, :], scalar=-1.0, in1=roots[:, 0, :], op0=MULT, op1=MULT)
             nc.vector.tensor_mul(out=coef[:], in0=part[:], in1=inv[:])
-            nc.tensor.transpose(sums[t][:, 3, :], coef[:], ident[:])
+            for j, term in enumerate((ones, coef)):
+                nc.tensor.matmul(out=sums[t][:, 3, :], lhsT=term[:], rhs=ident[:], is_transpose=True, start=(j == 0), stop=(j == 1))
 
         def guide(t):
             dn = sb([P, S], F32, f"dn{t}")
@@ -197,23 +200,20 @@ def tile_picked_yapgui_mom_p_kernel(
             nc.vector.scalar_tensor_tensor(
                 out=patch(kept[:]),
                 in0=sums[t][:, 3, :].unsqueeze(2).to_broadcast([P, V, D]),
-                scalar=1.0,
+                scalar=unit_sb[:, t : t + 1],
                 in1=patch(ec[t][:]),
-                op0=ADD,
+                op0=MULT,
                 op1=MULT,
             )
-            nc.vector.scalar_tensor_tensor(
-                out=own[:, t, :], in0=kept[:], scalar=unit_sb[:, t : t + 1], in1=dn[:], op0=MULT, op1=ADD
-            )
+            adder = nc.vector if t == PACK - 1 else nc.gpsimd
+            adder.tensor_add(out=own[:, t, :], in0=kept[:], in1=dn[:])
 
-        for t in range(PACK + 1):
-            if t < PACK:
-                patch_sums(t)
-            if t == PACK:
-                guide(0)
-            if t > 0:
-                factors(t - 1)
-        for t in range(1, PACK):
+        stages = (products, difference, patch_sums, factors)
+        for step in range(1, PACK + len(stages) - 1):
+            for lag, stage in enumerate(stages):
+                if 0 <= step - lag < PACK:
+                    stage(step - lag)
+        for t in range(PACK):
             guide(t)
 
         for h in range(CHUNKS):

@@ -2,7 +2,6 @@ import math
 from contextlib import ExitStack
 
 import concourse.mybir as mybir
-from concourse.masks import make_identity
 
 K, T, S, D, N, H = 1024, 2048, 512, 4, 256, 512
 FLOPS = 2 * (2 * K * H * S + H * N * S)
@@ -30,8 +29,8 @@ CHUNKS = 4
 SC = S // CHUNKS
 
 
-def load_scale_rows(queue, tile, scales):
-    for q in range(4):
+def load_scale_rows(queue, tile, scales, quadrants=range(4)):
+    for q in quadrants:
         queue.dma_start(
             out=tile[32 * q : 32 * q + 4, :, :].bitcast(I32),
             in_=scales[:, 4 * q : 4 * q + 4, :].rearrange("o r c -> r o c").bitcast(I32),
@@ -55,32 +54,46 @@ def tile_picked_yapgui_mom_p_kernel(
         xs_raw = sb([P, T], U8, "xs_raw")
         ws_raw = sb([P, 2, PASSES, H], U8, "ws_raw")
         ww_raw = sb([P, 2, PASSES, 2 * H], U8, "ww_raw")
-        xw_raw = [reused.tile([P, T], I32, name=f"xw_raw{o}", align_bytes=64, offset=4 * T * o) for o in range(PASSES)]
+        blank = reused.tile([P, P], F32, name="blank", align_bytes=64, offset=0)
         xs = [sb([P, S], U8, f"xs{o}") for o in range(PASSES)]
         unit15 = sb([P, PACK], F32, "unit15")
         ident = sb([P, P], F32, "ident")
         ones = sb([P, P], F32, "ones")
         warm = sb([P, 1], F32, "warm")
 
-        def load_words(o):
-            nc.gpsimd.dma_start(out=xw_raw[o][:], in_=x_words[o].rearrange("p c r -> p (c r)").bitcast(I32))
-
-        load_words(0)
-        make_identity(nc, ident[:])
-        nc.scalar.activation(out=warm[:], in_=ident[:, 0:1], func=ACT.Abs_reciprocal_sqrt, bias=0.1)
-        nc.gpsimd.memset(ones[:], 1.0)
-        nc.gpsimd.memset(xs[1][:].bitcast(I32), 0)
-        load_words(1)
         nc.vector.memset(xs_raw[:].bitcast(I32), 0)
-        nc.vector.memset(ws_raw[:].rearrange("p w o c -> p (w o c)").bitcast(I32), 0)
+        nc.vector.memset(ws_raw[:, 0].rearrange("p o c -> p (o c)").bitcast(I32), 0)
+        nc.gpsimd.memset(ws_raw[:, 1].rearrange("p o c -> p (o c)").bitcast(I32), 0)
+        nc.gpsimd.memset(xs[1][:].bitcast(I32), 0)
+        nc.gpsimd.memset(ones[:], 1.0)
+        nc.gpsimd.memset(blank[:], 0.0)
+        nc.gpsimd.affine_select(
+            out=ident[:],
+            in_=blank[:],
+            compare_op=mybir.AluOpType.not_equal,
+            fill=1.0,
+            base=0,
+            pattern=[[-1, P]],
+            channel_multiplier=1,
+        )
+        nc.scalar.activation(out=warm[:], in_=ident[:, 0:1], func=ACT.Abs_reciprocal_sqrt, bias=0.1)
+        load_scale_rows(nc.gpsimd, ws_raw[:, 1], w2_scales, (2, 3))
+
+        xw_raw = reused.tile([P, PASSES, T], I32, name="xw_raw", align_bytes=64, offset=0)
+
+        def load_words(o):
+            nc.sync.dma_start(out=xw_raw[:, o, :], in_=x_words[o].rearrange("p c r -> p (c r)").bitcast(I32))
+
         nc.sync.dma_start(offs_sb[:], offs)
         for w, words in enumerate((w1_words, w2_words)):
             nc.sync.dma_start(out=ww_raw[:, w].bitcast(I32), in_=words.rearrange("o p c -> p o c").bitcast(I32))
+        nc.sync.dma_start(mom_sb[:], mom)
         for q in range(4):
             nc.sync.dma_start(out=xs_raw[32 * q : 32 * q + 8, :].bitcast(I32), in_=x_scales[:, 4 * q : 4 * q + 4, :].bitcast(I32))
+        load_words(0)
         load_scale_rows(nc.sync, ws_raw[:, 0], w1_scales)
-        load_scale_rows(nc.sync, ws_raw[:, 1], w2_scales)
-        nc.sync.dma_start(mom_sb[:], mom)
+        load_scale_rows(nc.sync, ws_raw[:, 1], w2_scales, (0, 1))
+        load_words(1)
 
         xw = {}
         ww = {}
@@ -117,13 +130,15 @@ def tile_picked_yapgui_mom_p_kernel(
 
         def gather_words(o, tag):
             xw[o] = sb([P, S], I32, f"xw{o}", tag=tag)
-            nc.vector.tensor_copy(out=xw[o][:].bitcast(U32), in_=xw_raw[o][:].bitcast(U32).indirect(offs_sb[:]))
+            nc.vector.tensor_copy(out=xw[o][:].bitcast(U32), in_=xw_raw[:, o, :].bitcast(U32).indirect(offs_sb[:]))
 
         deal_words(0)
         nc.vector.tensor_copy(out=xs[0][:], in_=xs_raw[:].indirect(offs_sb[:]))
         for q in range(4):
             nc.scalar.dma_start(out=xs[1][32 * q : 32 * q + 4, :].bitcast(I32), in_=xs[0][32 * q + 4 : 32 * q + 8, :].bitcast(I32))
         gather_words(0, "xs_raw")
+        nc.vector.tensor_copy(out=ws[:], in_=ws_raw[:].rearrange("p w o (m t) -> p t (w o) m", t=PACK))
+        gather_words(1, "ws_raw")
         unit_sb = reused.tile([P, PACK], F32, name="unit_sb", align_bytes=64, offset=0)
         w3_sb = reused.tile([P, 2 * N], U8, name="w3_sb", align_bytes=64, offset=64)
         w3s_sb = reused.tile([P, 1, N], U8, name="w3s_sb", align_bytes=64, offset=64 + 2 * N)
@@ -132,8 +147,6 @@ def tile_picked_yapgui_mom_p_kernel(
         nc.gpsimd.memset(w3s_sb[:].rearrange("p o c -> p (o c)").bitcast(I32), 0)
         load_scale_rows(nc.sync, w3s_sb, w3_scales)
         nc.gpsimd.tensor_scalar(out=unit15[:], in0=unit_sb[:], scalar1=1.5, scalar2=0.0, op0=MULT, op1=ADD)
-        nc.vector.tensor_copy(out=ws[:], in_=ws_raw[:].rearrange("p w o (m t) -> p t (w o) m", t=PACK))
-        gather_words(1, "ws_raw")
         for o in range(PASSES):
             for w in range(2):
                 multiply(0, w, o)

import math
from contextlib import ExitStack

import concourse.mybir as mybir

K, T, S, D, N, H = 1024, 2048, 512, 4, 256, 512
FLOPS = 2 * (2 * K * H * S + H * N * S)

F32 = mybir.dt.float32
BF16 = mybir.dt.bfloat16
I32 = mybir.dt.int32
U32 = mybir.dt.uint32
U16 = mybir.dt.uint16
U8 = mybir.dt.uint8
FP8X4 = mybir.dt.float8_e4m3fn_x4
FP4X4 = mybir.dt.float4_e2m1fn_x4
ACT = mybir.ActivationFunctionType
MULT = mybir.AluOpType.mult
ADD = mybir.AluOpType.add

P = 128
PACK = 4
PASSES = K // (P * PACK)
V = S // D
HALVES = 2
SH = S // HALVES
LIST_COLS = SH // 16
CHUNKS = 4
SC = S // CHUNKS


def load_scale_rows(queue, tile, scales, quadrants=range(4)):
    for q in quadrants:
        queue.dma_start(
            out=tile[32 * q : 32 * q + 4, :, :].bitcast(I32),
            in_=scales[:, 4 * q : 4 * q + 4, :].rearrange("o r c -> r o c").bitcast(I32),
        )


def tile_picked_yapgui_mom_p_kernel(
    tc, x_words, x_scales, w1_words, w1_scales, w2_words, w2_scales, unit, w3_words, w3_scales, offs, mom, out
):
    nc = tc.nc
    with ExitStack() as ctx:
        keep = ctx.enter_context(tc.tile_pool(name="keep", bufs=1))
        reused = ctx.enter_context(tc.tile_pool(name="reused", bufs=1))
        psum = ctx.enter_context(tc.psum_pool(name="psum", bufs=1))

        def sb(shape, dtype, name, tag=None):
            return keep.tile(shape, dtype, name=name, tag=tag or name, align_bytes=64)

        offs_sb = keep.tile([P, S // 16], U16, name="offs_sb")
        mom_sb = keep.tile([P, S // 16], U16, name="mom_sb")
        xs_raw = sb([P, T], U8, "xs_raw")
        ws_raw = sb([P, 2, PASSES, H], U8, "ws_raw")
        ww_raw = sb([P, 2, PASSES, 2 * H], U8, "ww_raw")
        blank = reused.tile([P, P], F32, name="blank", align_bytes=64, offset=0)
        xs = [sb([P, S], U8, f"xs{o}") for o in range(PASSES)]
        unit15 = sb([P, PACK], F32, "unit15")
        ident = sb([P, P], F32, "ident")
        ones = sb([P, P], F32, "ones")
        warm = sb([P, 1], F32, "warm")

        nc.vector.memset(xs_raw[:].bitcast(I32), 0)
        nc.vector.memset(ws_raw[:, 0].rearrange("p o c -> p (o c)").bitcast(I32), 0)
        nc.gpsimd.memset(ws_raw[:, 1].rearrange("p o c -> p (o c)").bitcast(I32), 0)
        nc.gpsimd.memset(xs[1][:].bitcast(I32), 0)
        nc.gpsimd.memset(ones[:], 1.0)
        nc.gpsimd.memset(blank[:], 0.0)
        nc.gpsimd.affine_select(
            out=ident[:],
            in_=blank[:],
            compare_op=mybir.AluOpType.not_equal,
            fill=1.0,
            base=0,
            pattern=[[-1, P]],
            channel_multiplier=1,
        )
        nc.scalar.activation(out=warm[:], in_=ident[:, 0:1], func=ACT.Abs_reciprocal_sqrt, bias=0.1)
        load_scale_rows(nc.gpsimd, ws_raw[:, 1], w2_scales, (2, 3))

        xw_raw = reused.tile([P, PASSES, T], I32, name="xw_raw", align_bytes=64, offset=0)

        def load_words(o):
            nc.sync.dma_start(out=xw_raw[:, o, :], in_=x_words[o].rearrange("p c r -> p (c r)").bitcast(I32))

        nc.sync.dma_start(offs_sb[:], offs)
        for w, words in enumerate((w1_words, w2_words)):
            nc.sync.dma_start(out=ww_raw[:, w].bitcast(I32), in_=words.rearrange("o p c -> p o c").bitcast(I32))
        nc.sync.dma_start(mom_sb[:], mom)
        for q in range(4):
            nc.sync.dma_start(out=xs_raw[32 * q : 32 * q + 8, :].bitcast(I32), in_=x_scales[:, 4 * q : 4 * q + 4, :].bitcast(I32))
        load_words(0)
        load_scale_rows(nc.sync, ws_raw[:, 0], w1_scales)
        load_scale_rows(nc.sync, ws_raw[:, 1], w2_scales, (0, 1))
        load_words(1)

        xw = {}
        ww = {}
        ws = sb([P, PACK, 2 * PASSES, P], U8, "ws")
        prod = [[psum.tile([P, S], F32, name=f"prod{t}_{w}", tag=f"bank{t}_{w}") for w in range(2)] for t in range(PACK)]

        def deal_words(t):
            shape = [P, 2 * PASSES, 2 * P]
            if t == 0:
                ww[t] = sb(shape, U8, f"ww{t}")
            else:
                ww[t] = reused.tile(shape, U8, name=f"ww{t}", align_bytes=64, offset=4 * T + t * 2 * PASSES * 2 * P)
            nc.vector.tensor_copy(
                out=ww[t][:].rearrange("p g (m b) -> p g m b", b=2),
                in_=ww_raw[:].rearrange("p w o (m t b) -> p t (w o) m b", t=PACK, b=2)[:, t],
            )

        def multiply(t, w, o):
            nc.tensor.matmul_mx(
                out=prod[t][w][:],
                lhsT=ww[t][:, PASSES * w + o, :].bitcast(FP4X4),
                lhsT_scale=ws[:, t, PASSES * w + o, :],
                rhs=xw[o][:].bitcast(FP8X4),
                rhs_scale=xs[o][:],
                start=(o == 0),
                stop=(o == PASSES - 1),
            )

        def products(t):
            deal_words(t)
            for w in range(2):
                for o in range(PASSES):
                    multiply(t, w, o)

        def gather_words(o, tag):
            xw[o] = sb([P, S], I32, f"xw{o}", tag=tag)
            nc.vector.tensor_copy(out=xw[o][:].bitcast(U32), in_=xw_raw[:, o, :].bitcast(U32).indirect(offs_sb[:]))

        deal_words(0)
        nc.vector.tensor_copy(out=xs[0][:], in_=xs_raw[:].indirect(offs_sb[:]))
        for q in range(4):
            nc.scalar.dma_start(out=xs[1][32 * q : 32 * q + 4, :].bitcast(I32), in_=xs[0][32 * q + 4 : 32 * q + 8, :].bitcast(I32))
        gather_words(0, "xs_raw")
        nc.vector.tensor_copy(out=ws[:], in_=ws_raw[:].rearrange("p w o (m t) -> p t (w o) m", t=PACK))
        gather_words(1, "ws_raw")
        unit_sb = reused.tile([P, PACK], F32, name="unit_sb", align_bytes=64, offset=0)
        w3_sb = reused.tile([P, 2 * N], U8, name="w3_sb", align_bytes=64, offset=64)
        w3s_sb = reused.tile([P, 1, N], U8, name="w3s_sb", align_bytes=64, offset=64 + 2 * N)
        nc.sync.dma_start(out=unit_sb[:], in_=unit.rearrange("(p t) o -> p (t o)", t=PACK))
        nc.sync.dma_start(out=w3_sb[:].bitcast(I32), in_=w3_words[0].bitcast(I32))
        nc.gpsimd.memset(w3s_sb[:].rearrange("p o c -> p (o c)").bitcast(I32), 0)
        load_scale_rows(nc.sync, w3s_sb, w3_scales)
        nc.gpsimd.tensor_scalar(out=unit15[:], in0=unit_sb[:], scalar1=1.5, scalar2=0.0, op0=MULT, op1=ADD)
        for o in range(PASSES):
            for w in range(2):
                multiply(0, w, o)

        ec = [sb([P, S], F32, f"ec{t}") for t in range(PACK)]
        dlt = [sb([P, S], F32, f"dlt{t}") for t in range(PACK)]
        own = sb([P, PACK, S], F32, "own")
        fetched = sb([P, PACK, S], F32, "fetched")
        sums, back = {}, {}

        def patch(ap):
            return ap.rearrange("p (v d) -> p v d", d=D)

        def difference(t):
            nc.scalar.copy(out=ec[t][:], in_=prod[t][0][:])
            nc.vector.tensor_sub(out=dlt[t][:], in0=ec[t][:], in1=prod[t][1][:])

        def patch_sums(t):
            terms = [sb([P, D, V], F32, f"terms{t}_{j}") for j in range(3)]
            nc.scalar.activation(
                out=terms[1][:], in_=prod[t][0][:].rearrange("p (v d) -> p d v", d=D), func=ACT.Square, scale=math.sqrt(1 / 3)
            )
            nc.scalar.activation(out=terms[0][:].rearrange("p d v -> p v d"), in_=patch(dlt[t][:]), func=ACT.Square, scale=0.5)
            nc.vector.tensor_mul(out=terms[2][:].rearrange("p d v -> p v d"), in0=patch(dlt[t][:]), in1=patch(ec[t][:]))
            sums[t] = psum.tile([P, 4, P], F32, name=f"sums{t}", tag=f"bank{t}_1")
            for j in (1, 2, 0):
                for d in range(D):
                    nc.tensor.matmul(
                        out=sums[t][:, j, :], lhsT=terms[j][:, d, :], rhs=ident[:], is_transpose=True, start=(d == 0), stop=(d == D - 1)
                    )

        def factors(t):
            roots = sb([P, 2, P], F32, f"roots{t}")
            inv = sb([P, P], F32, f"inv{t}")
            part = sb([P, P], F32, f"part{t}")
            coef = sb([P, P], F32, f"coef{t}")
            nc.scalar.activation(out=roots[:], in_=sums[t][:, 0:2, :], func=ACT.Abs_reciprocal_sqrt, bias=0.1)
            nc.scalar.activation(out=inv[:], in_=roots[:, 1, :], func=ACT.Square, scale=math.sqrt(1.1 / 3))
            back[t] = psum.tile([P, P], F32, name=f"back{t}", tag=f"bank{t}_0")
            nc.tensor.transpose(back[t][:], roots[:, 0, :], ident[:])
            nc.vector.scalar_tensor_tensor(out=part[:], in0=sums[t][:, 2, :], scalar=-1.0, in1=roots[:, 0, :], op0=MULT, op1=MULT)
            nc.vector.tensor_mul(out=coef[:], in0=part[:], in1=inv[:])
            for j, term in enumerate((ones, coef)):
                nc.tensor.matmul(out=sums[t][:, 3, :], lhsT=term[:], rhs=ident[:], is_transpose=True, start=(j == 0), stop=(j == 1))

        def guide(t):
            dn = sb([P, S], F32, f"dn{t}")
            kept = sb([P, S], F32, f"kept{t}")
            nc.vector.scalar_tensor_tensor(
                out=patch(dn[:]),
                in0=back[t][:].unsqueeze(2).to_broadcast([P, V, D]),
                scalar=unit15[:, t : t + 1],
                in1=patch(dlt[t][:]),
                op0=MULT,
                op1=MULT,
            )
            for h in range(HALVES):
                nc.scalar.activation(
                    out=fetched[:, t, h * SH : (h + 1) * SH],
                    in_=dn[:].indirect(mom_sb[:, h * LIST_COLS : (h + 1) * LIST_COLS]),
                    func=ACT.Copy,
                    scale=-0.7 / 1.5,
                )
            nc.vector.scalar_tensor_tensor(
                out=patch(kept[:]),
                in0=sums[t][:, 3, :].unsqueeze(2).to_broadcast([P, V, D]),
                scalar=unit_sb[:, t : t + 1],
                in1=patch(ec[t][:]),
                op0=MULT,
                op1=MULT,
            )
            adder = nc.vector if t == PACK - 1 else nc.gpsimd
            adder.tensor_add(out=own[:, t, :], in0=kept[:], in1=dn[:])

        stages = (products, difference, patch_sums, factors)
        for step in range(1, PACK + len(stages) - 1):
            for lag, stage in enumerate(stages):
                if 0 <= step - lag < PACK:
                    stage(step - lag)
        for t in range(PACK):
            guide(t)

        for h in range(CHUNKS):
            cols = slice(h * SC, (h + 1) * SC)
            hid = sb([P, SC, PACK], BF16, f"hid{h}")
            codes = sb([P, SC], U32, f"codes{h}")
            scales = sb([P, SC], U8, f"scales{h}")
            res = sb([P, N // P, SC], F32, f"res{h}")
            nc.vector.tensor_add(
                out=hid[:].rearrange("p (c i) t -> p c t i", i=4),
                in0=own[:, :, cols].rearrange("p t (c i) -> p c t i", i=4),
                in1=fetched[:, :, cols].rearrange("p t (c i) -> p c t i", i=4),
            )
            nc.vector.quantize_mx(out=codes[:].bitcast(FP8X4), scales=scales[:], in_=hid[:].rearrange("p c t -> p (c t)"))
            acc = psum.tile([P, N // P, SC], F32, name=f"acc{h}", tag=f"bank{h}_0")
            for m in range(N // P):
                nc.tensor.matmul_mx(
                    out=acc[:, m, :],
                    lhsT=w3_sb[:, 2 * P * m : 2 * P * (m + 1)].bitcast(FP4X4),
                    lhsT_scale=w3s_sb[:, 0, P * m : P * (m + 1)],
                    rhs=codes[:].bitcast(FP8X4),
                    rhs_scale=scales[:],
                    start=True,
                    stop=True,
                )
            nc.scalar.copy(out=res[:], in_=acc[:])
            nc.sync.dma_start(out=out.rearrange("(m p) j -> p m j", p=P)[:, :, cols], in_=res[:])
